import numpy as np, ml_dtypes
CORES = [0,1,2,3]
N = 4
ROOT = 2
def setup_inputs(rng):
    return {"x": rng.standard_normal((N, 128, 128), dtype=np.float32).astype(ml_dtypes.bfloat16)}
def reference(x):
    y = np.full(x.shape, np.nan, x.dtype)
    y[ROOT] = x.max(axis=0)
    return {"y": y}

@@ -1,0 +1,38 @@
+from concourse.bass import DstId, RemoteDMATransfer
+
+SCRATCH = {
+    "own": ("sbuf", [128, 128], "bfloat16"),
+    "in0": ("sbuf", [128, 128], "bfloat16"),
+    "in2": ("sbuf", [128, 128], "bfloat16"),
+    "in3": ("sbuf", [128, 128], "bfloat16"),
+    "land": ("sbuf", [128, 128], "bfloat16"),
+}
+SEMAPHORES = ["loaded", "sent", "arrived", "done", "stored"]
+
+FOLDER = 1
+
+
+def rank_program(g, core, T, topo):
+    rank = T.rank_of(core)
+    if rank is None:
+        return
+    root = T.cores[2]
+    g.dma_start(T.own[:], T.x[:]).then_inc(T.sem.loaded, 16)
+    g.wait_ge(T.sem.loaded, 16)
+    if core != FOLDER:
+        rid, pid, _se = topo.addr(FOLDER)
+        g.remote_dma(T["in%d" % core][:], T.own[:], T.sem.arrived, T.sem.sent, pid, rid, topo.mask(core, FOLDER))
+        g.wait_ge(T.sem.sent, 16)
+    else:
+        g.wait_ge(T.sem.arrived, 48)
+        rid, pid, _se = topo.addr(root)
+        g.remote_dma_fused(
+            [RemoteDMATransfer(dst_ids=[DstId(rid=rid, pnc=pid)], dma_engine_mask=topo.mask(core, root),
+                               remote_sem=T.sem.done, srcs=[T.own[:], T.in0[:], T.in2[:], T.in3[:]],
+                               dsts=[T.land[:]], alu_op=2)],
+            local_sem=T.sem.sent)
+        g.wait_ge(T.sem.sent, 16)
+    if core == root:
+        g.wait_ge(T.sem.done, 16)
+        g.dma_start(T.y[:], T.land[:]).then_inc(T.sem.stored, 16)
+        g.wait_ge(T.sem.stored, 16)

@@ -1,38 +1,54 @@
 from concourse.bass import DstId, RemoteDMATransfer
 
-SCRATCH = {
-    "own": ("sbuf", [128, 128], "bfloat16"),
-    "in0": ("sbuf", [128, 128], "bfloat16"),
-    "in2": ("sbuf", [128, 128], "bfloat16"),
-    "in3": ("sbuf", [128, 128], "bfloat16"),
-    "land": ("sbuf", [128, 128], "bfloat16"),
-}
-SEMAPHORES = ["loaded", "sent", "arrived", "done", "stored"]
+Q = 4
+HELPER = 4
+MAX = 2
+QUAD = [0x000F, 0x00F0, 0x0F00, 0xF000]
 
-FOLDER = 1
+SCRATCH = {
+    "own": ("dram", [Q, 128, 32], "bfloat16"),
+    "inb": ("dram", [Q, 128, 32], "bfloat16"),
+    "land": ("dram", [Q, 128, 32], "bfloat16"),
+}
+SEMAPHORES = ["loaded", "arrived", "sent", "done", "stored"]
 
 
 def rank_program(g, core, T, topo):
     rank = T.rank_of(core)
-    if rank is None:
+    root = T.cores[T.root]
+    folder = [HELPER if c == root else c for c in T.cores]
+    if rank is None and core != HELPER:
         return
-    root = T.cores[2]
-    g.dma_start(T.own[:], T.x[:]).then_inc(T.sem.loaded, 16)
-    g.wait_ge(T.sem.loaded, 16)
-    if core != FOLDER:
-        rid, pid, _se = topo.addr(FOLDER)
-        g.remote_dma(T["in%d" % core][:], T.own[:], T.sem.arrived, T.sem.sent, pid, rid, topo.mask(core, FOLDER))
-        g.wait_ge(T.sem.sent, 16)
-    else:
-        g.wait_ge(T.sem.arrived, 48)
-        rid, pid, _se = topo.addr(root)
+
+    def dst_id(c):
+        rid, pid, _se = topo.addr(c)
+        return DstId(rid=rid, pnc=pid)
+
+    sent = 0
+    if rank is not None:
+        g.sync.dma_start(T.own[:], T.x[:]).then_inc(T.sem.loaded, 16)
+        g.wait_ge(T.sem.loaded, 16)
+        spread = [
+            RemoteDMATransfer(dst_ids=[dst_id(folder[q])], dma_engine_mask=QUAD[q], remote_sem=T.sem.arrived,
+                              src=T.own[q], dst=T.inb[rank])
+            for q in range(Q) if folder[q] != core
+        ]
+        g.remote_dma_fused(spread, local_sem=T.sem.sent)
+        sent += 4 * len(spread)
+
+    if core in folder:
+        q = folder.index(core)
+        srcs = [T.own[q] if r == rank else T.inb[r] for r in range(len(T.cores))]
+        g.wait_ge(T.sem.arrived, 4 * sum(1 for r in range(len(T.cores)) if r != rank))
         g.remote_dma_fused(
-            [RemoteDMATransfer(dst_ids=[DstId(rid=rid, pnc=pid)], dma_engine_mask=topo.mask(core, root),
-                               remote_sem=T.sem.done, srcs=[T.own[:], T.in0[:], T.in2[:], T.in3[:]],
-                               dsts=[T.land[:]], alu_op=2)],
+            [RemoteDMATransfer(dst_ids=[dst_id(root)], dma_engine_mask=topo.mask(core, root), remote_sem=T.sem.done,
+                               srcs=srcs, dsts=[T.land[q]], alu_op=MAX)],
             local_sem=T.sem.sent)
-        g.wait_ge(T.sem.sent, 16)
+        sent += 16
+
     if core == root:
-        g.wait_ge(T.sem.done, 16)
-        g.dma_start(T.y[:], T.land[:]).then_inc(T.sem.stored, 16)
-        g.wait_ge(T.sem.stored, 16)
+        g.sync.wait_ge(T.sem.done, 16 * Q)
+        g.sync.dma_start(T.y[:], T.land[:]).then_inc(T.sem.stored, 16)
+        g.sync.wait_ge(T.sem.stored, 16)
+
+    g.wait_ge(T.sem.sent, sent)

from concourse.bass import DstId, RemoteDMATransfer

Q = 4
HELPER = 4
MAX = 2
QUAD = [0x000F, 0x00F0, 0x0F00, 0xF000]

SCRATCH = {
    "own": ("dram", [Q, 128, 32], "bfloat16"),
    "inb": ("dram", [Q, 128, 32], "bfloat16"),
    "land": ("dram", [Q, 128, 32], "bfloat16"),
}
SEMAPHORES = ["loaded", "arrived", "sent", "done", "stored"]


def rank_program(g, core, T, topo):
    rank = T.rank_of(core)
    root = T.cores[T.root]
    folder = [HELPER if c == root else c for c in T.cores]
    if rank is None and core != HELPER:
        return

    def dst_id(c):
        rid, pid, _se = topo.addr(c)
        return DstId(rid=rid, pnc=pid)

    sent = 0
    if rank is not None:
        g.sync.dma_start(T.own[:], T.x[:]).then_inc(T.sem.loaded, 16)
        g.wait_ge(T.sem.loaded, 16)
        spread = [
            RemoteDMATransfer(dst_ids=[dst_id(folder[q])], dma_engine_mask=QUAD[q], remote_sem=T.sem.arrived,
                              src=T.own[q], dst=T.inb[rank])
            for q in range(Q) if folder[q] != core
        ]
        g.remote_dma_fused(spread, local_sem=T.sem.sent)
        sent += 4 * len(spread)

    if core in folder:
        q = folder.index(core)
        srcs = [T.own[q] if r == rank else T.inb[r] for r in range(len(T.cores))]
        g.wait_ge(T.sem.arrived, 4 * sum(1 for r in range(len(T.cores)) if r != rank))
        g.remote_dma_fused(
            [RemoteDMATransfer(dst_ids=[dst_id(root)], dma_engine_mask=topo.mask(core, root), remote_sem=T.sem.done,
                               srcs=srcs, dsts=[T.land[q]], alu_op=MAX)],
            local_sem=T.sem.sent)
        sent += 16

    if core == root:
        g.sync.wait_ge(T.sem.done, 16 * Q)
        g.sync.dma_start(T.y[:], T.land[:]).then_inc(T.sem.stored, 16)
        g.sync.wait_ge(T.sem.stored, 16)

    g.wait_ge(T.sem.sent, sent)
